import numpy as np
import ml_dtypes


def mxq(x, axis, fmt="e4m3"):
    dtype, down = {"e4m3": (ml_dtypes.float8_e4m3fn, 7), "e5m2": (ml_dtypes.float8_e5m2, 14)}[fmt]
    v = np.moveaxis(np.asarray(x, np.float32).astype(ml_dtypes.bfloat16).astype(np.float64), axis, -1)
    blocks = v.reshape(v.shape[:-1] + (-1, 32))
    amax = np.abs(blocks).max(-1, keepdims=True)
    byte = np.maximum(np.where(amax > 0, np.frexp(amax)[1] - 1 + 127, 0) - down, 1)
    scale = np.exp2(byte - 127.0)
    codes = (blocks / scale).astype(np.float32).astype(dtype).astype(np.float64)
    return np.moveaxis((codes * scale).reshape(v.shape), -1, axis)


WIDE = False


def mx_kscale(k):
    if not WIDE:
        return np.ones(k)
    levels = np.array([10, -10, 5, -5, 0])
    if k % 512:
        return np.exp2(np.random.permutation(np.resize(levels, k // 32))).repeat(32)
    a = np.empty((k // 512, 16))
    for p in range(k // 512):
        a[p, :8] = np.random.permutation(np.resize(levels, 8))
        for g in range(8):
            far = levels[np.abs(levels - a[p, g]) >= 10]
            a[p, g + 8] = far[np.random.randint(len(far))]
    return np.exp2(a.ravel()).repeat(32)


def f64(x):
    return np.asarray(x).astype(np.float64)


def striped(idx):
    return np.tile(idx.reshape(-1, 16).T, (8, 1)).astype(np.uint16)


def unstriped(offs):
    return offs[:16].T.reshape(-1).astype(np.int64)


def pack_weight(w):
    k, n = w.shape
    w = f64(np.asarray(w, np.float32).astype(ml_dtypes.bfloat16)).reshape(k // 32, 32, n)
    amax = np.abs(w).max(1)
    byte = np.clip(np.where(amax > 0, np.frexp(amax)[1] - 1 + 127 - 7, 1), 1, 254)
    scaled = (w * np.exp2(127.0 - byte)[:, None, :]).reshape(k, n).astype(np.float32)
    words = np.ascontiguousarray(scaled.reshape(k // 512, 128, 4, n).transpose(0, 1, 3, 2)).astype(ml_dtypes.float8_e4m3fn).view(np.uint8)
    return words, np.ascontiguousarray(byte.astype(np.uint8).reshape(k // 512, 16, n))


def unpack_weight(words, scales):
    g, p, n, _ = words.shape
    vals = np.ascontiguousarray(words).view(ml_dtypes.float8_e4m3fn).astype(np.float64) * np.repeat(np.exp2(scales.astype(np.float64) - 127.0), 8, axis=1)[..., None]
    return vals.transpose(0, 1, 3, 2).reshape(g * 512, n)


def sigmoid(v):
    return 1.0 / (1.0 + np.exp(-np.maximum(v, -700.0)))


K, T, S, D, N, H, V, U = 512, 2048, 1024, 4, 128, 512, 256, 512


def setup_inputs():
    n = np.random.standard_normal
    s = mx_kscale(K)[:, None]
    u = mx_kscale(H)
    packed_xT = pack_weight(n((K, T)) * s)
    return {
        "x_words": packed_xT[0],
        "x_scales": packed_xT[1],
        "w1": (n((K, H)) / np.sqrt(K) / s).astype(np.float32),
        "w2": (n((K, H)) / np.sqrt(K) / s).astype(np.float32),
        "mask": (np.random.uniform(0.2, 1.0, (H, S))).astype(np.float32),
        "unit": (np.random.uniform(0.6, 1.4, (H, 1)) * u[:, None]).astype(np.float32),
        "w3": (n((H, N)) / np.sqrt(H) / u[:, None]).astype(np.float32),
        "offs": striped(np.random.permutation(T)[:S]),
        "exp_": striped(np.random.permutation(S)),
        "per": striped(np.random.permutation(np.concatenate([np.arange(V), np.random.randint(0, V, U - V)]))),
    }


def reference(x_words, x_scales, w1, w2, mask, unit, w3, offs, exp_, per):
    xq = unpack_weight(x_words, x_scales)[:, unstriped(offs)]
    inf = mxq(f64(w1), 0, "e4m3").T @ xq
    load = np.log(np.exp(inf) + 1.0)
    ie = load[:, unstriped(exp_)]
    dose = ie * f64(mask)
    sus = mxq(f64(w2), 0, "e4m3").T @ xq
    susc = sigmoid(sus)
    haz = (dose / (dose + 1.0)) * susc
    toth = haz.reshape(len(haz), -1, D).sum(axis=2)
    pinf = -1.0 * np.exp(-1.0 * toth) + 1.0
    pp = pinf[:, unstriped(per)]
    shr = haz / (np.repeat(toth, D, axis=1) + 0.1)
    s2 = (shr) ** 2
    cnc = s2.reshape(len(s2), -1, D).sum(axis=2)
    cp = cnc[:, unstriped(per)]
    hid = f64(unit) * (pp - cp)
    return mxq(f64(w3), 0, "e4m3").T @ mxq(hid, 0, "e4m3")

@@ -1,0 +1,222 @@
+from contextlib import ExitStack
+
+import concourse.mybir as mybir
+
+K, T, S, D, N, H, V, U = 512, 2048, 1024, 4, 128, 512, 256, 512
+FLOPS = 2 * K * H * S * 2 + 2 * H * N * U
+
+F32 = mybir.dt.float32
+BF16 = mybir.dt.bfloat16
+U32 = mybir.dt.uint32
+I32 = mybir.dt.int32
+U16 = mybir.dt.uint16
+U8 = mybir.dt.uint8
+FP8X4 = mybir.dt.float8_e4m3fn_x4
+ALU = mybir.AluOpType
+ACT = mybir.ActivationFunctionType
+
+P = 128
+PACK = 4
+HALF = 512
+HALVES = S // HALF
+LIST_COLS = HALF // 16
+PIECE = 256
+PIECE_ORDER = (0, 2, 1, 3)
+LN_FLOOR = 2.0 ** -60
+
+
+def tile_picked_yepitpr_conc_p_kernel(
+    tc, x_words, x_scales, w1, w2, mask, unit, w3, offs, exp_, per, out
+):
+    nc = tc.nc
+    with ExitStack() as ctx:
+        keep = ctx.enter_context(tc.tile_pool(name="keep", bufs=1))
+        psum = ctx.enter_context(tc.psum_pool(name="psum", bufs=1))
+
+        def sb(name, shape, dtype, tag=None):
+            return keep.tile(shape, dtype, name=name, tag=tag or name, align_bytes=64)
+
+        def bank(name, b):
+            return psum.tile([P, HALF], F32, name=name, tag="bank%d" % b)
+
+        halves = [slice(h * HALF, (h + 1) * HALF) for h in range(HALVES)]
+        list_halves = [slice(h * LIST_COLS, (h + 1) * LIST_COLS) for h in range(HALVES)]
+
+        offs_sb = sb("offs_sb", [P, S // 16], U16)
+        exp_sb = sb("exp_sb", [P, S // 16], U16)
+        per_sb = sb("per_sb", [P, U // 16], U16)
+        xw = sb("xw", [P, T], U32)
+        xs = sb("xs", [P, T], U8)
+        w1_raw = sb("w1_raw", [P, PACK, H], F32)
+        w2_raw = sb("w2_raw", [P, PACK, H], F32)
+
+        nc.gpsimd.memset(xs[:].bitcast(I32), 0)
+        nc.sync.dma_start(w1_raw[:], w1.rearrange("(p j) c -> p j c", j=PACK))
+        for q in range(4):
+            nc.sync.dma_start(xs[32 * q : 32 * q + 4, :].bitcast(I32), x_scales[0, 4 * q : 4 * q + 4, :].bitcast(I32))
+        nc.sync.dma_start(offs_sb[:], offs)
+        nc.sync.dma_start(xw[:].bitcast(I32), x_words[0].rearrange("p n t -> p (n t)").bitcast(I32))
+        nc.sync.dma_start(w2_raw[:], w2.rearrange("(p j) c -> p j c", j=PACK))
+        nc.sync.dma_start(exp_sb[:], exp_)
+        nc.sync.dma_start(per_sb[:], per)
+
+        floor_col = sb("floor_col", [P, 1], F32)
+        one_col = sb("one_col", [P, 1], F32)
+        nc.gpsimd.memset(floor_col[:], LN_FLOOR)
+        nc.gpsimd.memset(one_col[:], 1.0)
+
+        gw = sb("gw", [P, S], U32)
+        gs = sb("gs", [P, S], U8)
+
+        def pick(piece):
+            cols = slice(piece * PIECE, (piece + 1) * PIECE)
+            entries = offs_sb[:, piece * PIECE // 16 : (piece + 1) * PIECE // 16]
+            nc.vector.tensor_copy(gw[:, cols], xw[:].indirect(entries))
+            nc.vector.tensor_copy(gs[:, cols], xs[:].indirect(entries))
+
+        def deal(engine_copy, dealt, raw, pair):
+            ts = slice(2 * pair, 2 * pair + 2)
+            engine_copy(
+                dealt[:].rearrange("p (t m j) -> p m t j", t=2, j=PACK),
+                raw[:].rearrange("p j (m t) -> p m t j", t=PACK)[:, :, ts, :],
+            )
+
+        def quantize(name, values, width):
+            codes = sb(name + "_codes", [P, width], U32)
+            scales = sb(name + "_scales", [P, width], U8)
+            nc.vector.quantize_mx(out=codes[:].bitcast(FP8X4), scales=scales[:], in_=values)
+            return codes, scales
+
+        def product(acc, weights, t, moving):
+            codes, scales = weights[t // 2]
+            cols = slice((t % 2) * P, (t % 2 + 1) * P)
+            nc.tensor.matmul_mx(
+                out=acc, lhsT=codes[:, cols].bitcast(FP8X4), lhsT_scale=scales[:, cols],
+                rhs=gw[:, moving].bitcast(FP8X4), rhs_scale=gs[:, moving], start=True, stop=True,
+            )
+
+        w1_bf = [sb("w1_bf%d" % a, [P, 2 * P * PACK], BF16) for a in range(2)]
+        for a in range(2):
+            deal(nc.vector.tensor_copy, w1_bf[a], w1_raw, a)
+        w1_q = [quantize("w1q%d" % a, w1_bf[a][:], 2 * P) for a in range(2)]
+
+        mask_rows = mask.rearrange("(p t) s -> p t s", t=PACK)
+        mask01 = sb("mask01", [P, 2, S], F32, tag="w1_raw")
+        nc.sync.dma_start(mask01[:], mask_rows[:, 0:2, :])
+        w3_raw = sb("w3_raw", [P, PACK, N], F32, tag="w1_bf0")
+        unit_sb = sb("unit_sb", [P, PACK], F32, tag="w1_bf1")
+        nc.sync.dma_start(w3_raw[:], w3.rearrange("(p j) c -> p j c", j=PACK))
+        nc.sync.dma_start(unit_sb[:], unit.rearrange("(p t) o -> p (t o)", t=PACK))
+
+        inf = [[bank("inf%d%d" % (t, h), 2 * t + h) for h in range(HALVES)] for t in range(PACK)]
+        sig = [sb("sig%d" % t, [P, S], F32, tag="ring%d" % t) for t in range(PACK)]
+        for piece in PIECE_ORDER:
+            pick(piece)
+            cols = slice(piece * PIECE, (piece + 1) * PIECE)
+            in_bank = slice(piece % 2 * PIECE, (piece % 2 + 1) * PIECE)
+            for t in range(PACK):
+                product(inf[t][piece // 2][:, in_bank], w1_q, t, cols)
+                nc.scalar.activation(sig[t][:, cols], inf[t][piece // 2][:, in_bank], ACT.Sigmoid, scale=-1.0)
+
+        w2_bf = [sb("w2_bf%d" % a, [P, 2 * P * PACK], BF16) for a in range(2)]
+        for a in range(2):
+            deal(nc.vector.tensor_copy, w2_bf[a], w2_raw, a)
+        w2_q = [quantize("w2q%d" % a, w2_bf[a][:], 2 * P) for a in range(2)]
+        mask23 = sb("mask23", [P, 2, S], F32, tag="w2_raw")
+        nc.sync.dma_start(mask23[:], mask_rows[:, 2:4, :])
+        mask_sb = [mask01, mask23]
+        w3_bf = sb("w3_bf", [P, N * PACK], BF16)
+        nc.vector.tensor_copy(w3_bf[:].rearrange("p (n j) -> p n j", j=PACK), w3_raw[:].rearrange("p j n -> p n j"))
+        w3_codes, w3_scales = quantize("w3q", w3_bf[:], N)
+        unit_neg = sb("unit_neg", [P, PACK], F32)
+        unit_100 = sb("unit_100", [P, PACK], F32)
+        nc.vector.tensor_scalar(unit_neg[:], unit_sb[:], -1.0, None, ALU.mult)
+        nc.vector.tensor_scalar(unit_100[:], unit_sb[:], 100.0, None, ALU.mult)
+
+        load = [sb("load%d" % t, [P, S], F32, tag="win%d" % t) for t in range(PACK)]
+        for t in range(PACK):
+            nc.scalar.activation(sig[t][:], sig[t][:], ACT.Ln, bias=floor_col[:])
+        for t in range(PACK):
+            for h in range(HALVES):
+                nc.vector.scalar_tensor_tensor(
+                    load[t][:, halves[h]], sig[t][:, halves[h]], -1.0, inf[t][h][:], ALU.mult, ALU.max
+                )
+
+        susc = [sb("susc%d" % t, [P, S], F32) for t in range(PACK)]
+        for t in range(PACK):
+            for h in range(HALVES):
+                sus = bank("sus%d%d" % (t, h), 2 * t + h)
+                product(sus[:], w2_q, t, halves[h])
+                nc.scalar.activation(susc[t][:, halves[h]], sus[:], ACT.Sigmoid)
+
+        dose_tags = ["ring3", "win0", "win1", "win2"]
+        dose = []
+        for t in range(PACK):
+            dose.append(sb("dose%d" % t, [P, S], F32, tag=dose_tags[t]))
+            for h in range(HALVES):
+                nc.vector.tensor_tensor(
+                    dose[t][:, halves[h]], load[t][:].indirect(exp_sb[:, list_halves[h]]),
+                    mask_sb[t // 2][:, t % 2, halves[h]], ALU.mult,
+                )
+        for t in range(PACK):
+            nc.scalar.activation(dose[t][:], dose[t][:], ACT.Ln, bias=one_col[:])
+        for t in range(PACK):
+            nc.scalar.activation(dose[t][:], dose[t][:], ACT.Exp, scale=-1.0)
+
+        haz = [sb("haz%d" % t, [P, S], F32) for t in range(PACK)]
+        sq = [sb("sq%d" % t, [P, S], F32) for t in range(PACK)]
+        toth = sb("toth", [P, PACK, V], F32)
+        ssq = sb("ssq", [P, PACK, V], F32)
+
+        def group_sum(name, total, values):
+            pairs = sb(name, [P, 2 * V], F32)
+            quad = values[:].rearrange("p (v a e) -> p v a e", a=2, e=2)
+            nc.vector.tensor_tensor(pairs[:].rearrange("p (v e) -> p v e", e=2), quad[:, :, 0, :], quad[:, :, 1, :], ALU.add)
+            two = pairs[:].rearrange("p (v e) -> p v e", e=2)
+            nc.vector.tensor_tensor(total, two[:, :, 0], two[:, :, 1], ALU.add)
+
+        for t in range(PACK):
+            nc.vector.scalar_tensor_tensor(haz[t][:], dose[t][:], 1.0, susc[t][:], ALU.subtract, ALU.mult)
+            group_sum("pair_h%d" % t, toth[:, t, :], haz[t])
+        for t in range(PACK):
+            nc.scalar.activation(sq[t][:], haz[t][:], ACT.Square)
+        for t in range(PACK):
+            group_sum("pair_q%d" % t, ssq[:, t, :], sq[t])
+
+        escape = sb("escape", [P, PACK, V], F32)
+        inv_sq = sb("inv_sq", [P, PACK, V], F32)
+        nc.scalar.activation(inv_sq[:], toth[:], ACT.Ln, bias=one_col[:], scale=-10.0)
+        for t in range(PACK):
+            nc.scalar.activation(inv_sq[:, t, :], inv_sq[:, t, :], ACT.Exp, scale=-2.0)
+            nc.scalar.activation(escape[:, t, :], toth[:, t, :], ACT.Exp)
+
+        planes = sb("planes", [P, PACK, U], BF16)
+        for t in range(PACK):
+            nc.vector.tensor_scalar(
+                escape[:, t, :], escape[:, t, :], unit_neg[:, t : t + 1], unit_sb[:, t : t + 1], ALU.mult, ALU.add
+            )
+            nc.vector.scalar_tensor_tensor(
+                ssq[:, t, :], inv_sq[:, t, :], unit_100[:, t : t + 1], ssq[:, t, :], ALU.mult, ALU.mult
+            )
+            nc.vector.tensor_tensor(sq[t][:, 0:V], escape[:, t, :], ssq[:, t, :], ALU.subtract)
+        for t in range(PACK):
+            looked_up = sq[t][:].indirect(per_sb[:])
+            if t < 2:
+                nc.scalar.activation(planes[:, t, :], looked_up, ACT.Copy)
+            else:
+                nc.vector.tensor_copy(planes[:, t, :], looked_up)
+
+        hid_bf = sb("hid_bf", [P, U * PACK], BF16)
+        nc.vector.tensor_copy(
+            hid_bf[:].rearrange("p (c i t) -> p c t i", i=4, t=PACK),
+            planes[:].rearrange("p t (c i) -> p c t i", i=4),
+        )
+        hid_codes, hid_scales = quantize("hidq", hid_bf[:], U)
+        regions = bank("regions", 0)
+        nc.tensor.matmul_mx(
+            out=regions[:], lhsT=w3_codes[:].bitcast(FP8X4), lhsT_scale=w3_scales[:],
+            rhs=hid_codes[:].bitcast(FP8X4), rhs_scale=hid_scales[:], start=True, stop=True,
+        )
+        result = sb("result", [P, U], F32)
+        nc.scalar.copy(result[:], regions[:])
+        nc.sync.dma_start(out, result[:])

@@ -1,6 +1,7 @@
 from contextlib import ExitStack
 
 import concourse.mybir as mybir
+from concourse.masks import make_identity
 
 K, T, S, D, N, H, V, U = 512, 2048, 1024, 4, 128, 512, 256, 512
 FLOPS = 2 * K * H * S * 2 + 2 * H * N * U
@@ -21,7 +22,6 @@ HALF = 512
 HALVES = S // HALF
 LIST_COLS = HALF // 16
 PIECE = 256
-PIECE_ORDER = (0, 2, 1, 3)
 LN_FLOOR = 2.0 ** -60
 
 
@@ -48,16 +48,25 @@ def tile_picked_yepitpr_conc_p_kernel(
         xw = sb("xw", [P, T], U32)
         xs = sb("xs", [P, T], U8)
         w1_raw = sb("w1_raw", [P, PACK, H], F32)
-        w2_raw = sb("w2_raw", [P, PACK, H], F32)
 
-        nc.gpsimd.memset(xs[:].bitcast(I32), 0)
-        nc.sync.dma_start(w1_raw[:], w1.rearrange("(p j) c -> p j c", j=PACK))
+        w2_raw = sb("w2_raw", [P, PACK, H], F32)
+        w3_raw = sb("w3_raw", [P, PACK, N], F32)
+        unit_sb = sb("unit_sb", [P, PACK], F32)
+        mask_sb = [sb("mask%d" % a, [P, 2, S], F32) for a in range(2)]
+        mask_rows = mask.rearrange("(p t) s -> p t s", t=PACK)
+
+        nc.vector.memset(xs[:].bitcast(I32), 0)
+        nc.sync.dma_start(offs_sb[:], offs)
+        nc.sync.dma_start(exp_sb[:], exp_)
+        nc.sync.dma_start(xw[:].bitcast(I32), x_words[0].rearrange("p n t -> p (n t)").bitcast(I32))
         for q in range(4):
             nc.sync.dma_start(xs[32 * q : 32 * q + 4, :].bitcast(I32), x_scales[0, 4 * q : 4 * q + 4, :].bitcast(I32))
-        nc.sync.dma_start(offs_sb[:], offs)
-        nc.sync.dma_start(xw[:].bitcast(I32), x_words[0].rearrange("p n t -> p (n t)").bitcast(I32))
+        nc.sync.dma_start(w1_raw[:], w1.rearrange("(p j) c -> p j c", j=PACK))
         nc.sync.dma_start(w2_raw[:], w2.rearrange("(p j) c -> p j c", j=PACK))
-        nc.sync.dma_start(exp_sb[:], exp_)
+        nc.sync.dma_start(w3_raw[:], w3.rearrange("(p j) c -> p j c", j=PACK))
+        nc.sync.dma_start(unit_sb[:], unit.rearrange("(p t) o -> p (t o)", t=PACK))
+        for a in range(2):
+            nc.sync.dma_start(mask_sb[a][:], mask_rows[:, 2 * a : 2 * a + 2, :])
         nc.sync.dma_start(per_sb[:], per)
 
         floor_col = sb("floor_col", [P, 1], F32)
@@ -65,20 +74,23 @@ def tile_picked_yepitpr_conc_p_kernel(
         nc.gpsimd.memset(floor_col[:], LN_FLOOR)
         nc.gpsimd.memset(one_col[:], 1.0)
 
-        gw = sb("gw", [P, S], U32)
-        gs = sb("gs", [P, S], U8)
+        ident = sb("ident", [P, P], F32)
+        make_identity(nc, ident[:])
 
-        def pick(piece):
-            cols = slice(piece * PIECE, (piece + 1) * PIECE)
-            entries = offs_sb[:, piece * PIECE // 16 : (piece + 1) * PIECE // 16]
-            nc.vector.tensor_copy(gw[:, cols], xw[:].indirect(entries))
-            nc.vector.tensor_copy(gs[:, cols], xs[:].indirect(entries))
+        def pick(words, scale_bytes, start, stop):
+            cols = slice(start % HALF, (stop - 1) % HALF + 1)
+            entries = offs_sb[:, start // 16 : stop // 16]
+            nc.vector.tensor_copy(words[:, cols], xw[:].indirect(entries))
+            nc.vector.tensor_copy(scale_bytes[:, cols], xs[:].indirect(entries))
 
-        def deal(engine_copy, dealt, raw, pair):
-            ts = slice(2 * pair, 2 * pair + 2)
-            engine_copy(
-                dealt[:].rearrange("p (t m j) -> p m t j", t=2, j=PACK),
-                raw[:].rearrange("p j (m t) -> p m t j", t=PACK)[:, :, ts, :],
+        gw = [sb("gw0", [P, HALF], U32)]
+        gs = [sb("gs0", [P, HALF], U8)]
+        pick(gw[0], gs[0], 0, HALF)
+
+        def deal(dealt, raw, first, count):
+            nc.vector.tensor_copy(
+                dealt[:].rearrange("p (t m j) -> p m t j", t=count, j=PACK),
+                raw[:].rearrange("p j (m t) -> p m t j", t=PACK)[:, :, first : first + count, :],
             )
 
         def quantize(name, values, width):
@@ -87,51 +99,45 @@ def tile_picked_yepitpr_conc_p_kernel(
             nc.vector.quantize_mx(out=codes[:].bitcast(FP8X4), scales=scales[:], in_=values)
             return codes, scales
 
-        def product(acc, weights, t, moving):
-            codes, scales = weights[t // 2]
-            cols = slice((t % 2) * P, (t % 2 + 1) * P)
+        def product(acc, weights, t, h, moving):
+            per_tile = PACK // len(weights)
+            codes, scales = weights[t // per_tile]
+            cols = slice((t % per_tile) * P, (t % per_tile + 1) * P)
             nc.tensor.matmul_mx(
                 out=acc, lhsT=codes[:, cols].bitcast(FP8X4), lhsT_scale=scales[:, cols],
-                rhs=gw[:, moving].bitcast(FP8X4), rhs_scale=gs[:, moving], start=True, stop=True,
+                rhs=gw[h][:, moving].bitcast(FP8X4), rhs_scale=gs[h][:, moving], start=True, stop=True,
             )
 
         w1_bf = [sb("w1_bf%d" % a, [P, 2 * P * PACK], BF16) for a in range(2)]
+        w1_q = []
         for a in range(2):
-            deal(nc.vector.tensor_copy, w1_bf[a], w1_raw, a)
-        w1_q = [quantize("w1q%d" % a, w1_bf[a][:], 2 * P) for a in range(2)]
-
-        mask_rows = mask.rearrange("(p t) s -> p t s", t=PACK)
-        mask01 = sb("mask01", [P, 2, S], F32, tag="w1_raw")
-        nc.sync.dma_start(mask01[:], mask_rows[:, 0:2, :])
-        w3_raw = sb("w3_raw", [P, PACK, N], F32, tag="w1_bf0")
-        unit_sb = sb("unit_sb", [P, PACK], F32, tag="w1_bf1")
-        nc.sync.dma_start(w3_raw[:], w3.rearrange("(p j) c -> p j c", j=PACK))
-        nc.sync.dma_start(unit_sb[:], unit.rearrange("(p t) o -> p (t o)", t=PACK))
+            deal(w1_bf[a], w1_raw, 2 * a, 2)
+            w1_q.append(quantize("w1q%d" % a, w1_bf[a][:], 2 * P))
 
         inf = [[bank("inf%d%d" % (t, h), 2 * t + h) for h in range(HALVES)] for t in range(PACK)]
         sig = [sb("sig%d" % t, [P, S], F32, tag="ring%d" % t) for t in range(PACK)]
-        for piece in PIECE_ORDER:
-            pick(piece)
-            cols = slice(piece * PIECE, (piece + 1) * PIECE)
-            in_bank = slice(piece % 2 * PIECE, (piece % 2 + 1) * PIECE)
+        for t in range(PACK):
+            product(inf[t][0][:], w1_q, t, 0, slice(0, HALF))
+            nc.scalar.activation(sig[t][:, halves[0]], inf[t][0][:], ACT.Sigmoid, scale=-1.0)
+        gw.append(sb("gw1", [P, HALF], U32, tag="w1_bf1"))
+        gs.append(sb("gs1", [P, HALF], U8, tag="w1_bf0"))
+        for part in range(2):
+            pick(gw[1], gs[1], HALF + part * PIECE, HALF + (part + 1) * PIECE)
+            in_bank = slice(part * PIECE, (part + 1) * PIECE)
+            cols = slice(HALF + part * PIECE, HALF + (part + 1) * PIECE)
             for t in range(PACK):
-                product(inf[t][piece // 2][:, in_bank], w1_q, t, cols)
-                nc.scalar.activation(sig[t][:, cols], inf[t][piece // 2][:, in_bank], ACT.Sigmoid, scale=-1.0)
+                product(inf[t][1][:, in_bank], w1_q, t, 1, in_bank)
+                nc.scalar.activation(sig[t][:, cols], inf[t][1][:, in_bank], ACT.Sigmoid, scale=-1.0)
 
         w2_bf = [sb("w2_bf%d" % a, [P, 2 * P * PACK], BF16) for a in range(2)]
         for a in range(2):
-            deal(nc.vector.tensor_copy, w2_bf[a], w2_raw, a)
+            deal(w2_bf[a], w2_raw, 2 * a, 2)
         w2_q = [quantize("w2q%d" % a, w2_bf[a][:], 2 * P) for a in range(2)]
-        mask23 = sb("mask23", [P, 2, S], F32, tag="w2_raw")
-        nc.sync.dma_start(mask23[:], mask_rows[:, 2:4, :])
-        mask_sb = [mask01, mask23]
         w3_bf = sb("w3_bf", [P, N * PACK], BF16)
         nc.vector.tensor_copy(w3_bf[:].rearrange("p (n j) -> p n j", j=PACK), w3_raw[:].rearrange("p j n -> p n j"))
         w3_codes, w3_scales = quantize("w3q", w3_bf[:], N)
         unit_neg = sb("unit_neg", [P, PACK], F32)
-        unit_100 = sb("unit_100", [P, PACK], F32)
         nc.vector.tensor_scalar(unit_neg[:], unit_sb[:], -1.0, None, ALU.mult)
-        nc.vector.tensor_scalar(unit_100[:], unit_sb[:], 100.0, None, ALU.mult)
 
         load = [sb("load%d" % t, [P, S], F32, tag="win%d" % t) for t in range(PACK)]
         for t in range(PACK):
@@ -146,8 +152,11 @@ def tile_picked_yepitpr_conc_p_kernel(
         for t in range(PACK):
             for h in range(HALVES):
                 sus = bank("sus%d%d" % (t, h), 2 * t + h)
-                product(sus[:], w2_q, t, halves[h])
-                nc.scalar.activation(susc[t][:, halves[h]], sus[:], ACT.Sigmoid)
+                product(sus[:], w2_q, t, h, slice(0, HALF))
+                nc.scalar.activation(
+                    susc[t][:].rearrange("p (d v) -> p d v", d=D)[:, :, h * P : (h + 1) * P],
+                    sus[:].rearrange("p (v d) -> p d v", d=D), ACT.Sigmoid,
+                )
 
         dose_tags = ["ring3", "win0", "win1", "win2"]
         dose = []
@@ -158,65 +167,88 @@ def tile_picked_yepitpr_conc_p_kernel(
                     dose[t][:, halves[h]], load[t][:].indirect(exp_sb[:, list_halves[h]]),
                     mask_sb[t // 2][:, t % 2, halves[h]], ALU.mult,
                 )
+        free = [sb("free%d" % t, [P, S], F32) for t in range(PACK)]
         for t in range(PACK):
-            nc.scalar.activation(dose[t][:], dose[t][:], ACT.Ln, bias=one_col[:])
+            nc.scalar.activation(
+                free[t][:].rearrange("p (d v) -> p v d", d=D), dose[t][:].rearrange("p (v d) -> p v d", d=D),
+                ACT.Ln, bias=one_col[:],
+            )
         for t in range(PACK):
-            nc.scalar.activation(dose[t][:], dose[t][:], ACT.Exp, scale=-1.0)
+            nc.scalar.activation(free[t][:], free[t][:], ACT.Exp, scale=-1.0)
 
         haz = [sb("haz%d" % t, [P, S], F32) for t in range(PACK)]
-        sq = [sb("sq%d" % t, [P, S], F32) for t in range(PACK)]
-        toth = sb("toth", [P, PACK, V], F32)
-        ssq = sb("ssq", [P, PACK, V], F32)
 
-        def group_sum(name, total, values):
-            pairs = sb(name, [P, 2 * V], F32)
-            quad = values[:].rearrange("p (v a e) -> p v a e", a=2, e=2)
-            nc.vector.tensor_tensor(pairs[:].rearrange("p (v e) -> p v e", e=2), quad[:, :, 0, :], quad[:, :, 1, :], ALU.add)
-            two = pairs[:].rearrange("p (v e) -> p v e", e=2)
-            nc.vector.tensor_tensor(total, two[:, :, 0], two[:, :, 1], ALU.add)
+        def turned_sum(total, values):
+            planes_d = values[:].rearrange("p (d b v) -> p d b v", d=D, v=P)
+            for b in range(V // P):
+                for dd in range(D):
+                    nc.tensor.matmul(
+                        total[:, b * P : (b + 1) * P], planes_d[:, dd, b, :], ident[:],
+                        start=(dd == 0), stop=(dd == D - 1), is_transpose=True,
+                    )
 
+        slots = [slice(t * V, (t + 1) * V) for t in range(PACK)]
+        pairs = [slice(2 * a * V, 2 * (a + 1) * V) for a in range(2)]
+        toth = [bank("toth%d" % a, a) for a in range(2)]
+        ssq = [bank("ssq%d" % a, 2 + a) for a in range(2)]
         for t in range(PACK):
-            nc.vector.scalar_tensor_tensor(haz[t][:], dose[t][:], 1.0, susc[t][:], ALU.subtract, ALU.mult)
-            group_sum("pair_h%d" % t, toth[:, t, :], haz[t])
+            nc.vector.scalar_tensor_tensor(haz[t][:], free[t][:], 1.0, susc[t][:], ALU.subtract, ALU.mult)
+            turned_sum(toth[t // 2][:, slots[t % 2]], haz[t])
+        sq_tags = ["free3", "haz0", "haz1", "haz2"]
+        sq = []
         for t in range(PACK):
-            nc.scalar.activation(sq[t][:], haz[t][:], ACT.Square)
-        for t in range(PACK):
-            group_sum("pair_q%d" % t, ssq[:, t, :], sq[t])
+            sq.append(sb("sq%d" % t, [P, S], F32, tag=sq_tags[t]))
+            nc.vector.tensor_tensor(sq[t][:], haz[t][:], haz[t][:], ALU.mult)
+            turned_sum(ssq[t // 2][:, slots[t % 2]], sq[t])
 
-        escape = sb("escape", [P, PACK, V], F32)
-        inv_sq = sb("inv_sq", [P, PACK, V], F32)
-        nc.scalar.activation(inv_sq[:], toth[:], ACT.Ln, bias=one_col[:], scale=-10.0)
+        log_sum = sb("log_sum", [P, PACK * V], F32)
+        conc = sb("conc", [P, PACK * V], F32)
+        for a in range(2):
+            nc.scalar.activation(log_sum[:, pairs[a]], toth[a][:], ACT.Ln, bias=one_col[:], scale=-10.0)
+        nc.scalar.activation(conc[:], log_sum[:], ACT.Exp, scale=-2.0)
+        escape = sb("escape", [P, PACK * V], F32, tag="log_sum")
+        for a in range(2):
+            nc.scalar.activation(escape[:, pairs[a]], toth[a][:], ACT.Exp)
+            nc.vector.scalar_tensor_tensor(conc[:, pairs[a]], conc[:, pairs[a]], 100.0, ssq[a][:], ALU.mult, ALU.mult)
         for t in range(PACK):
-            nc.scalar.activation(inv_sq[:, t, :], inv_sq[:, t, :], ACT.Exp, scale=-2.0)
-            nc.scalar.activation(escape[:, t, :], toth[:, t, :], ACT.Exp)
-
-        planes = sb("planes", [P, PACK, U], BF16)
-        for t in range(PACK):
-            nc.vector.tensor_scalar(
-                escape[:, t, :], escape[:, t, :], unit_neg[:, t : t + 1], unit_sb[:, t : t + 1], ALU.mult, ALU.add
-            )
-            nc.vector.scalar_tensor_tensor(
-                ssq[:, t, :], inv_sq[:, t, :], unit_100[:, t : t + 1], ssq[:, t, :], ALU.mult, ALU.mult
-            )
-            nc.vector.tensor_tensor(sq[t][:, 0:V], escape[:, t, :], ssq[:, t, :], ALU.subtract)
-        for t in range(PACK):
-            looked_up = sq[t][:].indirect(per_sb[:])
+            back = bank("back%d" % t, 4 + t)
+            for k, term in enumerate((escape, conc)):
+                for b in range(V // P):
+                    nc.tensor.matmul(
+                        back[:, b * P : (b + 1) * P], term[:, t * V + b * P : t * V + (b + 1) * P], ident[:],
+                        start=(k == 0 and b == 0), stop=(k == 1 and b == V // P - 1), is_transpose=True,
+                    )
             if t < 2:
-                nc.scalar.activation(planes[:, t, :], looked_up, ACT.Copy)
+                nc.scalar.activation(
+                    sq[t][:, 0:V], back[:, 0:V], ACT.Identity, bias=unit_sb[:, t : t + 1], scale=unit_neg[:, t : t + 1]
+                )
             else:
-                nc.vector.tensor_copy(planes[:, t, :], looked_up)
+                nc.vector.tensor_scalar(
+                    sq[t][:, 0:V], back[:, 0:V], unit_neg[:, t : t + 1], unit_sb[:, t : t + 1], ALU.mult, ALU.add
+                )
 
-        hid_bf = sb("hid_bf", [P, U * PACK], BF16)
-        nc.vector.tensor_copy(
-            hid_bf[:].rearrange("p (c i t) -> p c t i", i=4, t=PACK),
-            planes[:].rearrange("p t (c i) -> p c t i", i=4),
-        )
-        hid_codes, hid_scales = quantize("hidq", hid_bf[:], U)
-        regions = bank("regions", 0)
-        nc.tensor.matmul_mx(
-            out=regions[:], lhsT=w3_codes[:].bitcast(FP8X4), lhsT_scale=w3_scales[:],
-            rhs=hid_codes[:].bitcast(FP8X4), rhs_scale=hid_scales[:], start=True, stop=True,
-        )
-        result = sb("result", [P, U], F32)
-        nc.scalar.copy(result[:], regions[:])
-        nc.sync.dma_start(out, result[:])
+        order = (0, 1, 2, 3)
+        PART = U // 2
+        planes = [sb("planes%d" % h, [P, PACK, PART], BF16) for h in range(2)]
+        for h in range(2):
+            for t in order:
+                looked_up = sq[t][:].indirect(per_sb[:, h * PART // 16 : (h + 1) * PART // 16])
+                if h == 0 and t >= 2:
+                    nc.vector.tensor_copy(planes[h][:, t, :], looked_up)
+                else:
+                    nc.scalar.activation(planes[h][:, t, :], looked_up, ACT.Copy)
+        for h in range(2):
+            hid_bf = sb("hid_bf%d" % h, [P, PART * PACK], BF16)
+            nc.vector.tensor_copy(
+                hid_bf[:].rearrange("p (c i t) -> p c t i", i=4, t=PACK),
+                planes[h][:].rearrange("p t (c i) -> p c t i", i=4),
+            )
+            hid_codes, hid_scales = quantize("hidq%d" % h, hid_bf[:], PART)
+            regions = bank("regions%d" % h, h)
+            nc.tensor.matmul_mx(
+                out=regions[:, 0:PART], lhsT=w3_codes[:].bitcast(FP8X4), lhsT_scale=w3_scales[:],
+                rhs=hid_codes[:].bitcast(FP8X4), rhs_scale=hid_scales[:], start=True, stop=True,
+            )
+            result = sb("result%d" % h, [P, PART], F32)
+            nc.scalar.copy(result[:], regions[:, 0:PART])
+            nc.sync.dma_start(out[:, h * PART : (h + 1) * PART], result[:])

@@ -22,6 +22,7 @@ HALF = 512
 HALVES = S // HALF
 LIST_COLS = HALF // 16
 PIECE = 256
+PART = U // 2
 LN_FLOOR = 2.0 ** -60
 
 
@@ -93,8 +94,8 @@ def tile_picked_yepitpr_conc_p_kernel(
                 raw[:].rearrange("p j (m t) -> p m t j", t=PACK)[:, :, first : first + count, :],
             )
 
-        def quantize(name, values, width):
-            codes = sb(name + "_codes", [P, width], U32)
+        def quantize(name, values, width, tag=None):
+            codes = sb(name + "_codes", [P, width], U32, tag=tag)
             scales = sb(name + "_scales", [P, width], U8)
             nc.vector.quantize_mx(out=codes[:].bitcast(FP8X4), scales=scales[:], in_=values)
             return codes, scales
@@ -132,7 +133,6 @@ def tile_picked_yepitpr_conc_p_kernel(
         w2_bf = [sb("w2_bf%d" % a, [P, 2 * P * PACK], BF16) for a in range(2)]
         for a in range(2):
             deal(w2_bf[a], w2_raw, 2 * a, 2)
-        w2_q = [quantize("w2q%d" % a, w2_bf[a][:], 2 * P) for a in range(2)]
         w3_bf = sb("w3_bf", [P, N * PACK], BF16)
         nc.vector.tensor_copy(w3_bf[:].rearrange("p (n j) -> p n j", j=PACK), w3_raw[:].rearrange("p j n -> p n j"))
         w3_codes, w3_scales = quantize("w3q", w3_bf[:], N)
@@ -142,45 +142,71 @@ def tile_picked_yepitpr_conc_p_kernel(
         load = [sb("load%d" % t, [P, S], F32, tag="win%d" % t) for t in range(PACK)]
         for t in range(PACK):
             nc.scalar.activation(sig[t][:], sig[t][:], ACT.Ln, bias=floor_col[:])
-        for t in range(PACK):
+
+        def softplus(t):
             for h in range(HALVES):
                 nc.vector.scalar_tensor_tensor(
                     load[t][:, halves[h]], sig[t][:, halves[h]], -1.0, inf[t][h][:], ALU.mult, ALU.max
                 )
 
-        susc = [sb("susc%d" % t, [P, S], F32) for t in range(PACK)]
-        for t in range(PACK):
-            for h in range(HALVES):
-                sus = bank("sus%d%d" % (t, h), 2 * t + h)
-                product(sus[:], w2_q, t, h, slice(0, HALF))
-                nc.scalar.activation(
-                    susc[t][:].rearrange("p (d v) -> p d v", d=D)[:, :, h * P : (h + 1) * P],
-                    sus[:].rearrange("p (v d) -> p d v", d=D), ACT.Sigmoid,
-                )
+        dose = [sb("dose%d" % t, [P, S], F32) for t in range(PACK)]
+        log_dose = [sb("log_dose%d" % t, [P, S], F32) for t in range(PACK)]
+        fetched = {t: sb("fetched%d" % t, [P, S], F32) for t in (1, 3)}
 
-        dose_tags = ["ring3", "win0", "win1", "win2"]
-        dose = []
-        for t in range(PACK):
-            dose.append(sb("dose%d" % t, [P, S], F32, tag=dose_tags[t]))
+        def fetch_masked(t):
             for h in range(HALVES):
                 nc.vector.tensor_tensor(
                     dose[t][:, halves[h]], load[t][:].indirect(exp_sb[:, list_halves[h]]),
                     mask_sb[t // 2][:, t % 2, halves[h]], ALU.mult,
                 )
-        free = [sb("free%d" % t, [P, S], F32) for t in range(PACK)]
-        for t in range(PACK):
-            nc.scalar.activation(
-                free[t][:].rearrange("p (d v) -> p v d", d=D), dose[t][:].rearrange("p (v d) -> p v d", d=D),
-                ACT.Ln, bias=one_col[:],
-            )
-        for t in range(PACK):
-            nc.scalar.activation(free[t][:], free[t][:], ACT.Exp, scale=-1.0)
 
+        def fetch(t):
+            for h in range(HALVES):
+                nc.scalar.activation(fetched[t][:, halves[h]], load[t][:].indirect(exp_sb[:, list_halves[h]]), ACT.Copy)
+
+        def apply_mask(t):
+            nc.vector.tensor_tensor(dose[t][:], fetched[t][:], mask_sb[t // 2][:, t % 2, :], ALU.mult)
+
+        def log1p(t):
+            nc.scalar.activation(log_dose[t][:], dose[t][:], ACT.Ln, bias=one_col[:])
+
+        softplus(0)
+        softplus(1)
+        fetch_masked(0)
+        fetch(1)
+        log1p(0)
+        softplus(2)
+        softplus(3)
+        fetch(3)
+        apply_mask(1)
+        fetch_masked(2)
+        apply_mask(3)
+        for t in range(1, PACK):
+            log1p(t)
+
+        w2_q = [quantize("w2q0", w2_bf[0][:], 2 * P, tag="fetched3"), quantize("w2q1", w2_bf[1][:], 2 * P, tag="w2_bf0")]
+        free_tags = ["dose3", "log_dose0", "log_dose1", "log_dose2"]
+        susc = [sb("susc%d" % t, [P, S], F32) for t in range(PACK)]
         haz = [sb("haz%d" % t, [P, S], F32) for t in range(PACK)]
+        free = []
+        for t in range(PACK):
+            free.append(sb("free%d" % t, [P, S], F32, tag=free_tags[t]))
+            nc.scalar.activation(free[t][:], log_dose[t][:], ACT.Exp, scale=-1.0)
+            nc.vector.tensor_scalar(
+                haz[t][:].rearrange("p (d v) -> p v d", d=D), free[t][:].rearrange("p (v d) -> p v d", d=D),
+                0.5, -0.5, ALU.mult, ALU.add,
+            )
+            for h in range(HALVES):
+                sus = bank("sus%d%d" % (t, h), 2 * t + h)
+                product(sus[:], w2_q, t, h, slice(0, HALF))
+                nc.scalar.activation(
+                    susc[t][:].rearrange("p (d v) -> p d v", d=D)[:, :, h * P : (h + 1) * P],
+                    sus[:].rearrange("p (v d) -> p d v", d=D), ACT.Tanh, scale=0.5,
+                )
 
-        def turned_sum(total, values):
+        def turned_sum(total, values, blocks):
             planes_d = values[:].rearrange("p (d b v) -> p d b v", d=D, v=P)
-            for b in range(V // P):
+            for b in blocks:
                 for dd in range(D):
                     nc.tensor.matmul(
                         total[:, b * P : (b + 1) * P], planes_d[:, dd, b, :], ident[:],
@@ -192,63 +218,81 @@ def tile_picked_yepitpr_conc_p_kernel(
         toth = [bank("toth%d" % a, a) for a in range(2)]
         ssq = [bank("ssq%d" % a, 2 + a) for a in range(2)]
         for t in range(PACK):
-            nc.vector.scalar_tensor_tensor(haz[t][:], free[t][:], 1.0, susc[t][:], ALU.subtract, ALU.mult)
-            turned_sum(toth[t // 2][:, slots[t % 2]], haz[t])
-        sq_tags = ["free3", "haz0", "haz1", "haz2"]
+            for b in range(V // P):
+                block = haz[t][:].rearrange("p (d v) -> p d v", d=D)[:, :, b * P : (b + 1) * P]
+                tanh_block = susc[t][:].rearrange("p (d v) -> p d v", d=D)[:, :, b * P : (b + 1) * P]
+                nc.vector.scalar_tensor_tensor(block, tanh_block, 1.0, block, ALU.add, ALU.mult)
+                turned_sum(toth[t // 2][:, slots[t % 2]], haz[t], [b])
         sq = []
         for t in range(PACK):
-            sq.append(sb("sq%d" % t, [P, S], F32, tag=sq_tags[t]))
+            sq.append(sb("sq%d" % t, [P, S], F32))
             nc.vector.tensor_tensor(sq[t][:], haz[t][:], haz[t][:], ALU.mult)
-            turned_sum(ssq[t // 2][:, slots[t % 2]], sq[t])
+            turned_sum(ssq[t // 2][:, slots[t % 2]], sq[t], range(V // P))
 
         log_sum = sb("log_sum", [P, PACK * V], F32)
         conc = sb("conc", [P, PACK * V], F32)
+        escape = sb("escape", [P, PACK * V], F32)
+        nc.scalar.activation(escape[:, pairs[0]], toth[0][:], ACT.Exp)
         for a in range(2):
             nc.scalar.activation(log_sum[:, pairs[a]], toth[a][:], ACT.Ln, bias=one_col[:], scale=-10.0)
-        nc.scalar.activation(conc[:], log_sum[:], ACT.Exp, scale=-2.0)
-        escape = sb("escape", [P, PACK * V], F32, tag="log_sum")
-        for a in range(2):
-            nc.scalar.activation(escape[:, pairs[a]], toth[a][:], ACT.Exp)
-            nc.vector.scalar_tensor_tensor(conc[:, pairs[a]], conc[:, pairs[a]], 100.0, ssq[a][:], ALU.mult, ALU.mult)
+        nc.scalar.activation(conc[:, pairs[0]], log_sum[:, pairs[0]], ACT.Exp, scale=-2.0)
+        nc.scalar.activation(escape[:, pairs[1]], toth[1][:], ACT.Exp)
+        nc.scalar.activation(conc[:, pairs[1]], log_sum[:, pairs[1]], ACT.Exp, scale=-2.0)
+        back = []
         for t in range(PACK):
-            back = bank("back%d" % t, 4 + t)
+            nc.vector.scalar_tensor_tensor(
+                conc[:, slots[t]], conc[:, slots[t]], 100.0, ssq[t // 2][:, slots[t % 2]], ALU.mult, ALU.mult
+            )
+            back.append(bank("back%d" % t, 4 + t))
             for k, term in enumerate((escape, conc)):
                 for b in range(V // P):
                     nc.tensor.matmul(
-                        back[:, b * P : (b + 1) * P], term[:, t * V + b * P : t * V + (b + 1) * P], ident[:],
+                        back[t][:, b * P : (b + 1) * P], term[:, t * V + b * P : t * V + (b + 1) * P], ident[:],
                         start=(k == 0 and b == 0), stop=(k == 1 and b == V // P - 1), is_transpose=True,
                     )
-            if t < 2:
-                nc.scalar.activation(
-                    sq[t][:, 0:V], back[:, 0:V], ACT.Identity, bias=unit_sb[:, t : t + 1], scale=unit_neg[:, t : t + 1]
-                )
-            else:
-                nc.vector.tensor_scalar(
-                    sq[t][:, 0:V], back[:, 0:V], unit_neg[:, t : t + 1], unit_sb[:, t : t + 1], ALU.mult, ALU.add
-                )
 
-        order = (0, 1, 2, 3)
-        PART = U // 2
         planes = [sb("planes%d" % h, [P, PACK, PART], BF16) for h in range(2)]
-        for h in range(2):
-            for t in order:
-                looked_up = sq[t][:].indirect(per_sb[:, h * PART // 16 : (h + 1) * PART // 16])
-                if h == 0 and t >= 2:
-                    nc.vector.tensor_copy(planes[h][:, t, :], looked_up)
-                else:
-                    nc.scalar.activation(planes[h][:, t, :], looked_up, ACT.Copy)
-        for h in range(2):
-            hid_bf = sb("hid_bf%d" % h, [P, PART * PACK], BF16)
-            nc.vector.tensor_copy(
-                hid_bf[:].rearrange("p (c i t) -> p c t i", i=4, t=PACK),
+        hid_bf = [sb("hid_bf%d" % h, [P, PART * PACK], BF16) for h in range(2)]
+
+        def look_up(t, h, on_scalar):
+            looked_up = sq[t][:].indirect(per_sb[:, h * PART // 16 : (h + 1) * PART // 16])
+            if on_scalar:
+                nc.scalar.activation(planes[h][:, t, :], looked_up, ACT.Copy)
+            else:
+                nc.vector.tensor_copy(planes[h][:, t, :], looked_up)
+
+        def interleave(h, copy):
+            copy(
+                hid_bf[h][:].rearrange("p (c i t) -> p c t i", i=4, t=PACK),
                 planes[h][:].rearrange("p t (c i) -> p c t i", i=4),
             )
-            hid_codes, hid_scales = quantize("hidq%d" % h, hid_bf[:], PART)
+
+        def last_product(h):
+            hid_codes, hid_scales = quantize("hidq%d" % h, hid_bf[h][:], PART)
             regions = bank("regions%d" % h, h)
             nc.tensor.matmul_mx(
                 out=regions[:, 0:PART], lhsT=w3_codes[:].bitcast(FP8X4), lhsT_scale=w3_scales[:],
                 rhs=hid_codes[:].bitcast(FP8X4), rhs_scale=hid_scales[:], start=True, stop=True,
             )
             result = sb("result%d" % h, [P, PART], F32)
-            nc.scalar.copy(result[:], regions[:, 0:PART])
+            if h == 0:
+                nc.scalar.copy(result[:], regions[:, 0:PART])
+            else:
+                nc.vector.tensor_copy(result[:], regions[:, 0:PART])
             nc.sync.dma_start(out[:, h * PART : (h + 1) * PART], result[:])
+
+        for t in range(PACK):
+            if t % 2 == 0:
+                nc.scalar.activation(
+                    sq[t][:, 0:V], back[t][:, 0:V], ACT.Identity, bias=unit_sb[:, t : t + 1], scale=unit_neg[:, t : t + 1]
+                )
+            else:
+                nc.vector.tensor_scalar(
+                    sq[t][:, 0:V], back[t][:, 0:V], unit_neg[:, t : t + 1], unit_sb[:, t : t + 1], ALU.mult, ALU.add
+                )
+            look_up(t, 0, t % 2 == 0)
+            look_up(t, 1, t != 1)
+        interleave(0, nc.vector.tensor_copy)
+        interleave(1, nc.scalar.copy)
+        last_product(0)
+        last_product(1)

@@ -4,7 +4,7 @@ import concourse.mybir as mybir
 from concourse.masks import make_identity
 
 K, T, S, D, N, H, V, U = 512, 2048, 1024, 4, 128, 512, 256, 512
-FLOPS = 2 * K * H * S * 2 + 2 * H * N * U
+FLOPS = 2 * (2 * K * H * S) + 2 * H * N * U
 
 F32 = mybir.dt.float32
 BF16 = mybir.dt.bfloat16
@@ -18,12 +18,16 @@ ACT = mybir.ActivationFunctionType
 
 P = 128
 PACK = 4
-HALF = 512
-HALVES = S // HALF
-LIST_COLS = HALF // 16
-PIECE = 256
+PAIRS = PACK // 2
+BANK = 512
+HALVES = S // BANK
+PIECE = BANK // 2
+BLOCKS = V // P
 PART = U // 2
-LN_FLOOR = 2.0 ** -60
+STRIPE = 16
+LINE = 4
+LN_FLOOR = 2.0**-60
+SCALAR_LANES = (1, 3)
 
 
 def tile_picked_yepitpr_conc_p_kernel(
@@ -34,265 +38,263 @@ def tile_picked_yepitpr_conc_p_kernel(
         keep = ctx.enter_context(tc.tile_pool(name="keep", bufs=1))
         psum = ctx.enter_context(tc.psum_pool(name="psum", bufs=1))
 
-        def sb(name, shape, dtype, tag=None):
+        def sbuf(name, shape, dtype, tag=None):
             return keep.tile(shape, dtype, name=name, tag=tag or name, align_bytes=64)
 
-        def bank(name, b):
-            return psum.tile([P, HALF], F32, name=name, tag="bank%d" % b)
+        def bank(name, number):
+            return psum.tile([P, BANK], F32, name=name, tag="bank%d" % number)
 
-        halves = [slice(h * HALF, (h + 1) * HALF) for h in range(HALVES)]
-        list_halves = [slice(h * LIST_COLS, (h + 1) * LIST_COLS) for h in range(HALVES)]
+        def span(index, width):
+            return slice(index * width, (index + 1) * width)
 
-        offs_sb = sb("offs_sb", [P, S // 16], U16)
-        exp_sb = sb("exp_sb", [P, S // 16], U16)
-        per_sb = sb("per_sb", [P, U // 16], U16)
-        xw = sb("xw", [P, T], U32)
-        xs = sb("xs", [P, T], U8)
-        w1_raw = sb("w1_raw", [P, PACK, H], F32)
+        def entries(list_tile, index, width):
+            return list_tile[:, span(index, width // STRIPE)]
 
-        w2_raw = sb("w2_raw", [P, PACK, H], F32)
-        w3_raw = sb("w3_raw", [P, PACK, N], F32)
-        unit_sb = sb("unit_sb", [P, PACK], F32)
-        mask_sb = [sb("mask%d" % a, [P, 2, S], F32) for a in range(2)]
-        mask_rows = mask.rearrange("(p t) s -> p t s", t=PACK)
+        def member_major(tile):
+            return tile[:].rearrange("p (d v) -> p d v", d=D)
 
-        nc.vector.memset(xs[:].bitcast(I32), 0)
-        nc.sync.dma_start(offs_sb[:], offs)
-        nc.sync.dma_start(exp_sb[:], exp_)
-        nc.sync.dma_start(xw[:].bitcast(I32), x_words[0].rearrange("p n t -> p (n t)").bitcast(I32))
-        for q in range(4):
-            nc.sync.dma_start(xs[32 * q : 32 * q + 4, :].bitcast(I32), x_scales[0, 4 * q : 4 * q + 4, :].bitcast(I32))
-        nc.sync.dma_start(w1_raw[:], w1.rearrange("(p j) c -> p j c", j=PACK))
-        nc.sync.dma_start(w2_raw[:], w2.rearrange("(p j) c -> p j c", j=PACK))
-        nc.sync.dma_start(w3_raw[:], w3.rearrange("(p j) c -> p j c", j=PACK))
-        nc.sync.dma_start(unit_sb[:], unit.rearrange("(p t) o -> p (t o)", t=PACK))
-        for a in range(2):
-            nc.sync.dma_start(mask_sb[a][:], mask_rows[:, 2 * a : 2 * a + 2, :])
-        nc.sync.dma_start(per_sb[:], per)
-
-        floor_col = sb("floor_col", [P, 1], F32)
-        one_col = sb("one_col", [P, 1], F32)
-        nc.gpsimd.memset(floor_col[:], LN_FLOOR)
-        nc.gpsimd.memset(one_col[:], 1.0)
-
-        ident = sb("ident", [P, P], F32)
-        make_identity(nc, ident[:])
-
-        def pick(words, scale_bytes, start, stop):
-            cols = slice(start % HALF, (stop - 1) % HALF + 1)
-            entries = offs_sb[:, start // 16 : stop // 16]
-            nc.vector.tensor_copy(words[:, cols], xw[:].indirect(entries))
-            nc.vector.tensor_copy(scale_bytes[:, cols], xs[:].indirect(entries))
-
-        gw = [sb("gw0", [P, HALF], U32)]
-        gs = [sb("gs0", [P, HALF], U8)]
-        pick(gw[0], gs[0], 0, HALF)
-
-        def deal(dealt, raw, first, count):
-            nc.vector.tensor_copy(
-                dealt[:].rearrange("p (t m j) -> p m t j", t=count, j=PACK),
-                raw[:].rearrange("p j (m t) -> p m t j", t=PACK)[:, :, first : first + count, :],
-            )
-
-        def quantize(name, values, width, tag=None):
-            codes = sb(name + "_codes", [P, width], U32, tag=tag)
-            scales = sb(name + "_scales", [P, width], U8)
-            nc.vector.quantize_mx(out=codes[:].bitcast(FP8X4), scales=scales[:], in_=values)
+        def quantize(name, packed, tag=None):
+            width = packed.shape[1] // PACK
+            codes = sbuf(name + "_codes", [P, width], U32, tag=tag)
+            scales = sbuf(name + "_scales", [P, width], U8)
+            nc.vector.quantize_mx(out=codes[:].bitcast(FP8X4), scales=scales[:], in_=packed[:])
             return codes, scales
 
-        def product(acc, weights, t, h, moving):
-            per_tile = PACK // len(weights)
-            codes, scales = weights[t // per_tile]
-            cols = slice((t % per_tile) * P, (t % per_tile + 1) * P)
+        def product(result, stationary, stationary_cols, moving, moving_cols):
             nc.tensor.matmul_mx(
-                out=acc, lhsT=codes[:, cols].bitcast(FP8X4), lhsT_scale=scales[:, cols],
-                rhs=gw[h][:, moving].bitcast(FP8X4), rhs_scale=gs[h][:, moving], start=True, stop=True,
+                out=result,
+                lhsT=stationary[0][:, stationary_cols].bitcast(FP8X4),
+                lhsT_scale=stationary[1][:, stationary_cols],
+                rhs=moving[0][:, moving_cols].bitcast(FP8X4),
+                rhs_scale=moving[1][:, moving_cols],
+                start=True,
+                stop=True,
             )
 
-        w1_bf = [sb("w1_bf%d" % a, [P, 2 * P * PACK], BF16) for a in range(2)]
-        w1_q = []
-        for a in range(2):
-            deal(w1_bf[a], w1_raw, 2 * a, 2)
-            w1_q.append(quantize("w1q%d" % a, w1_bf[a][:], 2 * P))
+        offs_sb = sbuf("offs_sb", [P, S // STRIPE], U16)
+        exp_sb = sbuf("exp_sb", [P, S // STRIPE], U16)
+        per_sb = sbuf("per_sb", [P, U // STRIPE], U16)
+        table_words = sbuf("table_words", [P, T], U32)
+        table_scales = sbuf("table_scales", [P, T], U8)
+        w1_raw = sbuf("w1_raw", [P, PACK, H], F32)
+        w2_raw = sbuf("w2_raw", [P, PACK, H], F32)
+        w3_raw = sbuf("w3_raw", [P, PACK, N], F32)
+        unit_sb = sbuf("unit_sb", [P, PACK], F32)
+        mask_sb = [sbuf("mask%d" % a, [P, 2, S], F32) for a in range(PAIRS)]
 
-        inf = [[bank("inf%d%d" % (t, h), 2 * t + h) for h in range(HALVES)] for t in range(PACK)]
-        sig = [sb("sig%d" % t, [P, S], F32, tag="ring%d" % t) for t in range(PACK)]
+        nc.vector.memset(table_scales[:].bitcast(I32), 0)
+        nc.sync.dma_start(offs_sb[:], offs)
+        nc.sync.dma_start(exp_sb[:], exp_)
+        nc.sync.dma_start(table_words[:].bitcast(I32), x_words[0].rearrange("p n t -> p (n t)").bitcast(I32))
+        for q in range(4):
+            nc.sync.dma_start(table_scales[32 * q : 32 * q + 4, :].bitcast(I32), x_scales[0, span(q, 4), :].bitcast(I32))
+        for raw, weight in ((w1_raw, w1), (w2_raw, w2), (w3_raw, w3)):
+            nc.sync.dma_start(raw[:], weight.rearrange("(p r) c -> p r c", r=PACK))
+        nc.sync.dma_start(unit_sb[:], unit.rearrange("(p t) o -> p (t o)", t=PACK))
+        for a in range(PAIRS):
+            nc.sync.dma_start(mask_sb[a][:], mask.rearrange("(p t) s -> p t s", t=PACK)[:, span(a, 2), :])
+        nc.sync.dma_start(per_sb[:], per)
+
+        floor_col = sbuf("floor_col", [P, 1], F32)
+        one_col = sbuf("one_col", [P, 1], F32)
+        nc.gpsimd.memset(floor_col[:], LN_FLOOR)
+        nc.gpsimd.memset(one_col[:], 1.0)
+        ident = sbuf("ident", [P, P], F32)
+        make_identity(nc, ident[:])
+
+        def pick(target, cols, list_cols):
+            nc.vector.tensor_copy(target[0][:, cols], table_words[:].indirect(list_cols))
+            nc.vector.tensor_copy(target[1][:, cols], table_scales[:].indirect(list_cols))
+
+        def deal(packed, raw, a):
+            nc.vector.tensor_copy(
+                packed[:].rearrange("p (u m r) -> p m u r", u=2, r=PACK),
+                raw[:].rearrange("p r (m t) -> p m t r", t=PACK)[:, :, span(a, 2), :],
+            )
+
+        whole = span(0, BANK)
+        picked = [(sbuf("picked_words0", [P, BANK], U32), sbuf("picked_scales0", [P, BANK], U8))]
+        pick(picked[0], whole, entries(offs_sb, 0, BANK))
+        w1_packed = [sbuf("w1_packed%d" % a, [P, 2 * P * PACK], BF16) for a in range(PAIRS)]
+        w1_mx = []
+        for a in range(PAIRS):
+            deal(w1_packed[a], w1_raw, a)
+            w1_mx.append(quantize("w1_mx%d" % a, w1_packed[a]))
+
+        inf = [[bank("inf%d%d" % (t, h), HALVES * t + h) for h in range(HALVES)] for t in range(PACK)]
+        log_sig = [sbuf("log_sig%d" % t, [P, S], F32) for t in range(PACK)]
         for t in range(PACK):
-            product(inf[t][0][:], w1_q, t, 0, slice(0, HALF))
-            nc.scalar.activation(sig[t][:, halves[0]], inf[t][0][:], ACT.Sigmoid, scale=-1.0)
-        gw.append(sb("gw1", [P, HALF], U32, tag="w1_bf1"))
-        gs.append(sb("gs1", [P, HALF], U8, tag="w1_bf0"))
-        for part in range(2):
-            pick(gw[1], gs[1], HALF + part * PIECE, HALF + (part + 1) * PIECE)
-            in_bank = slice(part * PIECE, (part + 1) * PIECE)
-            cols = slice(HALF + part * PIECE, HALF + (part + 1) * PIECE)
+            product(inf[t][0][:], w1_mx[t // 2], span(t % 2, P), picked[0], whole)
+            nc.scalar.activation(log_sig[t][:, whole], inf[t][0][:], ACT.Sigmoid, scale=-1.0)
+        picked.append(
+            (sbuf("picked_words1", [P, BANK], U32, tag="w1_packed1"), sbuf("picked_scales1", [P, BANK], U8, tag="w1_packed0"))
+        )
+        for piece in range(BANK // PIECE):
+            in_half = span(piece, PIECE)
+            piece_of_list = BANK // PIECE + piece
+            pick(picked[1], in_half, entries(offs_sb, piece_of_list, PIECE))
             for t in range(PACK):
-                product(inf[t][1][:, in_bank], w1_q, t, 1, in_bank)
-                nc.scalar.activation(sig[t][:, cols], inf[t][1][:, in_bank], ACT.Sigmoid, scale=-1.0)
+                product(inf[t][1][:, in_half], w1_mx[t // 2], span(t % 2, P), picked[1], in_half)
+                nc.scalar.activation(log_sig[t][:, span(piece_of_list, PIECE)], inf[t][1][:, in_half], ACT.Sigmoid, scale=-1.0)
 
-        w2_bf = [sb("w2_bf%d" % a, [P, 2 * P * PACK], BF16) for a in range(2)]
-        for a in range(2):
-            deal(w2_bf[a], w2_raw, 2 * a, 2)
-        w3_bf = sb("w3_bf", [P, N * PACK], BF16)
-        nc.vector.tensor_copy(w3_bf[:].rearrange("p (n j) -> p n j", j=PACK), w3_raw[:].rearrange("p j n -> p n j"))
-        w3_codes, w3_scales = quantize("w3q", w3_bf[:], N)
-        unit_neg = sb("unit_neg", [P, PACK], F32)
+        w2_packed = [sbuf("w2_packed%d" % a, [P, 2 * P * PACK], BF16) for a in range(PAIRS)]
+        for a in range(PAIRS):
+            deal(w2_packed[a], w2_raw, a)
+        w3_packed = sbuf("w3_packed", [P, N * PACK], BF16)
+        nc.vector.tensor_copy(w3_packed[:].rearrange("p (c r) -> p c r", r=PACK), w3_raw[:].rearrange("p r c -> p c r"))
+        w3_mx = quantize("w3_mx", w3_packed)
+        unit_neg = sbuf("unit_neg", [P, PACK], F32)
         nc.vector.tensor_scalar(unit_neg[:], unit_sb[:], -1.0, None, ALU.mult)
 
-        load = [sb("load%d" % t, [P, S], F32, tag="win%d" % t) for t in range(PACK)]
+        load = [sbuf("load%d" % t, [P, S], F32) for t in range(PACK)]
         for t in range(PACK):
-            nc.scalar.activation(sig[t][:], sig[t][:], ACT.Ln, bias=floor_col[:])
+            nc.scalar.activation(log_sig[t][:], log_sig[t][:], ACT.Ln, bias=floor_col[:])
+        dose = [sbuf("dose%d" % t, [P, S], F32) for t in range(PACK)]
+        log_dose = [sbuf("log_dose%d" % t, [P, S], F32) for t in range(PACK)]
+        fetched = {t: sbuf("fetched%d" % t, [P, S], F32) for t in SCALAR_LANES}
 
         def softplus(t):
             for h in range(HALVES):
-                nc.vector.scalar_tensor_tensor(
-                    load[t][:, halves[h]], sig[t][:, halves[h]], -1.0, inf[t][h][:], ALU.mult, ALU.max
-                )
-
-        dose = [sb("dose%d" % t, [P, S], F32) for t in range(PACK)]
-        log_dose = [sb("log_dose%d" % t, [P, S], F32) for t in range(PACK)]
-        fetched = {t: sb("fetched%d" % t, [P, S], F32) for t in (1, 3)}
-
-        def fetch_masked(t):
-            for h in range(HALVES):
-                nc.vector.tensor_tensor(
-                    dose[t][:, halves[h]], load[t][:].indirect(exp_sb[:, list_halves[h]]),
-                    mask_sb[t // 2][:, t % 2, halves[h]], ALU.mult,
-                )
+                cols = span(h, BANK)
+                nc.vector.scalar_tensor_tensor(load[t][:, cols], log_sig[t][:, cols], -1.0, inf[t][h][:], ALU.mult, ALU.max)
 
         def fetch(t):
             for h in range(HALVES):
-                nc.scalar.activation(fetched[t][:, halves[h]], load[t][:].indirect(exp_sb[:, list_halves[h]]), ACT.Copy)
+                cols = span(h, BANK)
+                looked_up = load[t][:].indirect(entries(exp_sb, h, BANK))
+                if t in SCALAR_LANES:
+                    nc.scalar.activation(fetched[t][:, cols], looked_up, ACT.Copy)
+                else:
+                    nc.vector.tensor_tensor(dose[t][:, cols], looked_up, mask_sb[t // 2][:, t % 2, cols], ALU.mult)
 
         def apply_mask(t):
             nc.vector.tensor_tensor(dose[t][:], fetched[t][:], mask_sb[t // 2][:, t % 2, :], ALU.mult)
 
-        def log1p(t):
+        def log_one_plus(t):
             nc.scalar.activation(log_dose[t][:], dose[t][:], ACT.Ln, bias=one_col[:])
 
         softplus(0)
         softplus(1)
-        fetch_masked(0)
+        fetch(0)
         fetch(1)
-        log1p(0)
+        log_one_plus(0)
         softplus(2)
         softplus(3)
         fetch(3)
         apply_mask(1)
-        fetch_masked(2)
+        fetch(2)
         apply_mask(3)
         for t in range(1, PACK):
-            log1p(t)
+            log_one_plus(t)
 
-        w2_q = [quantize("w2q0", w2_bf[0][:], 2 * P, tag="fetched3"), quantize("w2q1", w2_bf[1][:], 2 * P, tag="w2_bf0")]
-        free_tags = ["dose3", "log_dose0", "log_dose1", "log_dose2"]
-        susc = [sb("susc%d" % t, [P, S], F32) for t in range(PACK)]
-        haz = [sb("haz%d" % t, [P, S], F32) for t in range(PACK)]
-        free = []
+        w2_mx = [quantize("w2_mx0", w2_packed[0], tag="fetched3"), quantize("w2_mx1", w2_packed[1], tag="w2_packed0")]
+        inv_dose_tags = ["dose%d" % (PACK - 1)] + ["log_dose%d" % t for t in range(PACK - 1)]
+        tanh_sus = [sbuf("tanh_sus%d" % t, [P, S], F32) for t in range(PACK)]
+        haz = [sbuf("haz%d" % t, [P, S], F32) for t in range(PACK)]
         for t in range(PACK):
-            free.append(sb("free%d" % t, [P, S], F32, tag=free_tags[t]))
-            nc.scalar.activation(free[t][:], log_dose[t][:], ACT.Exp, scale=-1.0)
+            inv_dose = sbuf("inv_dose%d" % t, [P, S], F32, tag=inv_dose_tags[t])
+            nc.scalar.activation(inv_dose[:], log_dose[t][:], ACT.Exp, scale=-1.0)
             nc.vector.tensor_scalar(
-                haz[t][:].rearrange("p (d v) -> p v d", d=D), free[t][:].rearrange("p (v d) -> p v d", d=D),
-                0.5, -0.5, ALU.mult, ALU.add,
+                haz[t][:].rearrange("p (d v) -> p v d", d=D),
+                inv_dose[:].rearrange("p (v d) -> p v d", d=D),
+                0.5,
+                -0.5,
+                ALU.mult,
+                ALU.add,
             )
             for h in range(HALVES):
-                sus = bank("sus%d%d" % (t, h), 2 * t + h)
-                product(sus[:], w2_q, t, h, slice(0, HALF))
+                sus = bank("sus%d%d" % (t, h), HALVES * t + h)
+                product(sus[:], w2_mx[t // 2], span(t % 2, P), picked[h], whole)
                 nc.scalar.activation(
-                    susc[t][:].rearrange("p (d v) -> p d v", d=D)[:, :, h * P : (h + 1) * P],
-                    sus[:].rearrange("p (v d) -> p d v", d=D), ACT.Tanh, scale=0.5,
+                    member_major(tanh_sus[t])[:, :, span(h, P)], sus[:].rearrange("p (v d) -> p d v", d=D), ACT.Tanh, scale=0.5
                 )
 
-        def turned_sum(total, values, blocks):
-            planes_d = values[:].rearrange("p (d b v) -> p d b v", d=D, v=P)
-            for b in blocks:
-                for dd in range(D):
-                    nc.tensor.matmul(
-                        total[:, b * P : (b + 1) * P], planes_d[:, dd, b, :], ident[:],
-                        start=(dd == 0), stop=(dd == D - 1), is_transpose=True,
-                    )
+        def turned_lane(pair_banks, t):
+            return pair_banks[t // 2][:, span(t % 2, V)]
 
-        slots = [slice(t * V, (t + 1) * V) for t in range(PACK)]
-        pairs = [slice(2 * a * V, 2 * (a + 1) * V) for a in range(2)]
-        toth = [bank("toth%d" % a, a) for a in range(2)]
-        ssq = [bank("ssq%d" % a, 2 + a) for a in range(2)]
-        for t in range(PACK):
-            for b in range(V // P):
-                block = haz[t][:].rearrange("p (d v) -> p d v", d=D)[:, :, b * P : (b + 1) * P]
-                tanh_block = susc[t][:].rearrange("p (d v) -> p d v", d=D)[:, :, b * P : (b + 1) * P]
-                nc.vector.scalar_tensor_tensor(block, tanh_block, 1.0, block, ALU.add, ALU.mult)
-                turned_sum(toth[t // 2][:, slots[t % 2]], haz[t], [b])
-        sq = []
-        for t in range(PACK):
-            sq.append(sb("sq%d" % t, [P, S], F32))
-            nc.vector.tensor_tensor(sq[t][:], haz[t][:], haz[t][:], ALU.mult)
-            turned_sum(ssq[t // 2][:, slots[t % 2]], sq[t], range(V // P))
+        def turned_sum(total, values, b):
+            for d in range(D):
+                nc.tensor.matmul(
+                    total[:, span(b, P)],
+                    member_major(values)[:, d, span(b, P)],
+                    ident[:],
+                    start=(d == 0),
+                    stop=(d == D - 1),
+                    is_transpose=True,
+                )
 
-        log_sum = sb("log_sum", [P, PACK * V], F32)
-        conc = sb("conc", [P, PACK * V], F32)
-        escape = sb("escape", [P, PACK * V], F32)
-        nc.scalar.activation(escape[:, pairs[0]], toth[0][:], ACT.Exp)
-        for a in range(2):
-            nc.scalar.activation(log_sum[:, pairs[a]], toth[a][:], ACT.Ln, bias=one_col[:], scale=-10.0)
-        nc.scalar.activation(conc[:, pairs[0]], log_sum[:, pairs[0]], ACT.Exp, scale=-2.0)
-        nc.scalar.activation(escape[:, pairs[1]], toth[1][:], ACT.Exp)
-        nc.scalar.activation(conc[:, pairs[1]], log_sum[:, pairs[1]], ACT.Exp, scale=-2.0)
+        toth = [bank("toth%d" % a, a) for a in range(PAIRS)]
+        square_sum = [bank("square_sum%d" % a, PAIRS + a) for a in range(PAIRS)]
+        for t in range(PACK):
+            for b in range(BLOCKS):
+                block = member_major(haz[t])[:, :, span(b, P)]
+                nc.vector.scalar_tensor_tensor(block, member_major(tanh_sus[t])[:, :, span(b, P)], 1.0, block, ALU.add, ALU.mult)
+                turned_sum(turned_lane(toth, t), haz[t], b)
+        square = [sbuf("square%d" % t, [P, S], F32) for t in range(PACK)]
+        for t in range(PACK):
+            nc.vector.tensor_tensor(square[t][:], haz[t][:], haz[t][:], ALU.mult)
+            for b in range(BLOCKS):
+                turned_sum(turned_lane(square_sum, t), square[t], b)
+
+        log_toth = sbuf("log_toth", [P, PACK * V], F32)
+        conc = sbuf("conc", [P, PACK * V], F32)
+        for a in range(PAIRS):
+            nc.scalar.activation(log_toth[:, span(a, 2 * V)], toth[a][:], ACT.Ln, bias=one_col[:], scale=-10.0)
+        nc.scalar.activation(conc[:], log_toth[:], ACT.Exp, scale=-2.0)
+        escape = sbuf("escape", [P, PACK * V], F32, tag="log_toth")
+        for a in range(PAIRS):
+            nc.scalar.activation(escape[:, span(a, 2 * V)], toth[a][:], ACT.Exp)
         back = []
         for t in range(PACK):
-            nc.vector.scalar_tensor_tensor(
-                conc[:, slots[t]], conc[:, slots[t]], 100.0, ssq[t // 2][:, slots[t % 2]], ALU.mult, ALU.mult
-            )
-            back.append(bank("back%d" % t, 4 + t))
-            for k, term in enumerate((escape, conc)):
-                for b in range(V // P):
+            lane = span(t, V)
+            nc.vector.scalar_tensor_tensor(conc[:, lane], conc[:, lane], 100.0, turned_lane(square_sum, t), ALU.mult, ALU.mult)
+            back.append(bank("back%d" % t, 2 * PAIRS + t))
+            for term_number, term in enumerate((conc, escape)):
+                for b in range(BLOCKS):
                     nc.tensor.matmul(
-                        back[t][:, b * P : (b + 1) * P], term[:, t * V + b * P : t * V + (b + 1) * P], ident[:],
-                        start=(k == 0 and b == 0), stop=(k == 1 and b == V // P - 1), is_transpose=True,
+                        back[t][:, span(b, P)],
+                        term[:, span(BLOCKS * t + b, P)],
+                        ident[:],
+                        start=(term_number == 0 and b == 0),
+                        stop=(term_number == 1 and b == BLOCKS - 1),
+                        is_transpose=True,
                     )
 
-        planes = [sb("planes%d" % h, [P, PACK, PART], BF16) for h in range(2)]
-        hid_bf = [sb("hid_bf%d" % h, [P, PART * PACK], BF16) for h in range(2)]
+        lane_values = [sbuf("lane_values%d" % h, [P, PACK, PART], BF16) for h in range(U // PART)]
+        hid_packed = [sbuf("hid_packed%d" % h, [P, PART * PACK], BF16) for h in range(U // PART)]
 
         def look_up(t, h, on_scalar):
-            looked_up = sq[t][:].indirect(per_sb[:, h * PART // 16 : (h + 1) * PART // 16])
+            looked_up = square[t][:].indirect(entries(per_sb, h, PART))
             if on_scalar:
-                nc.scalar.activation(planes[h][:, t, :], looked_up, ACT.Copy)
+                nc.scalar.activation(lane_values[h][:, t, :], looked_up, ACT.Copy)
             else:
-                nc.vector.tensor_copy(planes[h][:, t, :], looked_up)
+                nc.vector.tensor_copy(lane_values[h][:, t, :], looked_up)
 
-        def interleave(h, copy):
-            copy(
-                hid_bf[h][:].rearrange("p (c i t) -> p c t i", i=4, t=PACK),
-                planes[h][:].rearrange("p t (c i) -> p c t i", i=4),
+        def interleave(h):
+            nc.vector.tensor_copy(
+                hid_packed[h][:].rearrange("p (c i t) -> p c t i", i=LINE, t=PACK),
+                lane_values[h][:].rearrange("p t (c i) -> p c t i", i=LINE),
             )
 
         def last_product(h):
-            hid_codes, hid_scales = quantize("hidq%d" % h, hid_bf[h][:], PART)
+            hid_mx = quantize("hid_mx%d" % h, hid_packed[h])
             regions = bank("regions%d" % h, h)
-            nc.tensor.matmul_mx(
-                out=regions[:, 0:PART], lhsT=w3_codes[:].bitcast(FP8X4), lhsT_scale=w3_scales[:],
-                rhs=hid_codes[:].bitcast(FP8X4), rhs_scale=hid_scales[:], start=True, stop=True,
-            )
-            result = sb("result%d" % h, [P, PART], F32)
-            if h == 0:
-                nc.scalar.copy(result[:], regions[:, 0:PART])
-            else:
-                nc.vector.tensor_copy(result[:], regions[:, 0:PART])
-            nc.sync.dma_start(out[:, h * PART : (h + 1) * PART], result[:])
+            product(regions[:, 0:PART], w3_mx, span(0, N), hid_mx, span(0, PART))
+            result = sbuf("result%d" % h, [P, PART], F32)
+            nc.scalar.copy(result[:], regions[:, 0:PART])
+            nc.sync.dma_start(out[:, span(h, PART)], result[:])
 
         for t in range(PACK):
+            factor, offset = unit_neg[:, t : t + 1], unit_sb[:, t : t + 1]
             if t % 2 == 0:
-                nc.scalar.activation(
-                    sq[t][:, 0:V], back[t][:, 0:V], ACT.Identity, bias=unit_sb[:, t : t + 1], scale=unit_neg[:, t : t + 1]
-                )
+                nc.scalar.activation(square[t][:, 0:V], back[t][:, 0:V], ACT.Identity, bias=offset, scale=factor)
             else:
-                nc.vector.tensor_scalar(
-                    sq[t][:, 0:V], back[t][:, 0:V], unit_neg[:, t : t + 1], unit_sb[:, t : t + 1], ALU.mult, ALU.add
-                )
+                nc.vector.tensor_scalar(square[t][:, 0:V], back[t][:, 0:V], factor, offset, ALU.mult, ALU.add)
             look_up(t, 0, t % 2 == 0)
-            look_up(t, 1, t != 1)
-        interleave(0, nc.vector.tensor_copy)
-        interleave(1, nc.scalar.copy)
+        interleave(0)
+        for t in (0, 2, 1):
+            look_up(t, 1, True)
+        look_up(PACK - 1, 1, False)
         last_product(0)
+        interleave(1)
         last_product(1)

from contextlib import ExitStack

import concourse.mybir as mybir
from concourse.masks import make_identity

K, T, S, D, N, H, V, U = 512, 2048, 1024, 4, 128, 512, 256, 512
FLOPS = 2 * (2 * K * H * S) + 2 * H * N * U

F32 = mybir.dt.float32
BF16 = mybir.dt.bfloat16
U32 = mybir.dt.uint32
I32 = mybir.dt.int32
U16 = mybir.dt.uint16
U8 = mybir.dt.uint8
FP8X4 = mybir.dt.float8_e4m3fn_x4
ALU = mybir.AluOpType
ACT = mybir.ActivationFunctionType

P = 128
PACK = 4
PAIRS = PACK // 2
BANK = 512
HALVES = S // BANK
PIECE = BANK // 2
BLOCKS = V // P
PART = U // 2
STRIPE = 16
LINE = 4
LN_FLOOR = 2.0**-60
SCALAR_LANES = (1, 3)


def tile_picked_yepitpr_conc_p_kernel(
    tc, x_words, x_scales, w1, w2, mask, unit, w3, offs, exp_, per, out
):
    nc = tc.nc
    with ExitStack() as ctx:
        keep = ctx.enter_context(tc.tile_pool(name="keep", bufs=1))
        psum = ctx.enter_context(tc.psum_pool(name="psum", bufs=1))

        def sbuf(name, shape, dtype, tag=None):
            return keep.tile(shape, dtype, name=name, tag=tag or name, align_bytes=64)

        def bank(name, number):
            return psum.tile([P, BANK], F32, name=name, tag="bank%d" % number)

        def span(index, width):
            return slice(index * width, (index + 1) * width)

        def entries(list_tile, index, width):
            return list_tile[:, span(index, width // STRIPE)]

        def member_major(tile):
            return tile[:].rearrange("p (d v) -> p d v", d=D)

        def quantize(name, packed, tag=None):
            width = packed.shape[1] // PACK
            codes = sbuf(name + "_codes", [P, width], U32, tag=tag)
            scales = sbuf(name + "_scales", [P, width], U8)
            nc.vector.quantize_mx(out=codes[:].bitcast(FP8X4), scales=scales[:], in_=packed[:])
            return codes, scales

        def product(result, stationary, stationary_cols, moving, moving_cols):
            nc.tensor.matmul_mx(
                out=result,
                lhsT=stationary[0][:, stationary_cols].bitcast(FP8X4),
                lhsT_scale=stationary[1][:, stationary_cols],
                rhs=moving[0][:, moving_cols].bitcast(FP8X4),
                rhs_scale=moving[1][:, moving_cols],
                start=True,
                stop=True,
            )

        offs_sb = sbuf("offs_sb", [P, S // STRIPE], U16)
        exp_sb = sbuf("exp_sb", [P, S // STRIPE], U16)
        per_sb = sbuf("per_sb", [P, U // STRIPE], U16)
        table_words = sbuf("table_words", [P, T], U32)
        table_scales = sbuf("table_scales", [P, T], U8)
        w1_raw = sbuf("w1_raw", [P, PACK, H], F32)
        w2_raw = sbuf("w2_raw", [P, PACK, H], F32)
        w3_raw = sbuf("w3_raw", [P, PACK, N], F32)
        unit_sb = sbuf("unit_sb", [P, PACK], F32)
        mask_sb = [sbuf("mask%d" % a, [P, 2, S], F32) for a in range(PAIRS)]

        nc.vector.memset(table_scales[:].bitcast(I32), 0)
        nc.sync.dma_start(offs_sb[:], offs)
        nc.sync.dma_start(exp_sb[:], exp_)
        nc.sync.dma_start(table_words[:].bitcast(I32), x_words[0].rearrange("p n t -> p (n t)").bitcast(I32))
        for q in range(4):
            nc.sync.dma_start(table_scales[32 * q : 32 * q + 4, :].bitcast(I32), x_scales[0, span(q, 4), :].bitcast(I32))
        for raw, weight in ((w1_raw, w1), (w2_raw, w2), (w3_raw, w3)):
            nc.sync.dma_start(raw[:], weight.rearrange("(p r) c -> p r c", r=PACK))
        nc.sync.dma_start(unit_sb[:], unit.rearrange("(p t) o -> p (t o)", t=PACK))
        for a in range(PAIRS):
            nc.sync.dma_start(mask_sb[a][:], mask.rearrange("(p t) s -> p t s", t=PACK)[:, span(a, 2), :])
        nc.sync.dma_start(per_sb[:], per)

        floor_col = sbuf("floor_col", [P, 1], F32)
        one_col = sbuf("one_col", [P, 1], F32)
        nc.gpsimd.memset(floor_col[:], LN_FLOOR)
        nc.gpsimd.memset(one_col[:], 1.0)
        ident = sbuf("ident", [P, P], F32)
        make_identity(nc, ident[:])

        def pick(target, cols, list_cols):
            nc.vector.tensor_copy(target[0][:, cols], table_words[:].indirect(list_cols))
            nc.vector.tensor_copy(target[1][:, cols], table_scales[:].indirect(list_cols))

        def deal(packed, raw, a):
            nc.vector.tensor_copy(
                packed[:].rearrange("p (u m r) -> p m u r", u=2, r=PACK),
                raw[:].rearrange("p r (m t) -> p m t r", t=PACK)[:, :, span(a, 2), :],
            )

        whole = span(0, BANK)
        picked = [(sbuf("picked_words0", [P, BANK], U32), sbuf("picked_scales0", [P, BANK], U8))]
        pick(picked[0], whole, entries(offs_sb, 0, BANK))
        w1_packed = [sbuf("w1_packed%d" % a, [P, 2 * P * PACK], BF16) for a in range(PAIRS)]
        w1_mx = []
        for a in range(PAIRS):
            deal(w1_packed[a], w1_raw, a)
            w1_mx.append(quantize("w1_mx%d" % a, w1_packed[a]))

        inf = [[bank("inf%d%d" % (t, h), HALVES * t + h) for h in range(HALVES)] for t in range(PACK)]
        log_sig = [sbuf("log_sig%d" % t, [P, S], F32) for t in range(PACK)]
        for t in range(PACK):
            product(inf[t][0][:], w1_mx[t // 2], span(t % 2, P), picked[0], whole)
            nc.scalar.activation(log_sig[t][:, whole], inf[t][0][:], ACT.Sigmoid, scale=-1.0)
        picked.append(
            (sbuf("picked_words1", [P, BANK], U32, tag="w1_packed1"), sbuf("picked_scales1", [P, BANK], U8, tag="w1_packed0"))
        )
        for piece in range(BANK // PIECE):
            in_half = span(piece, PIECE)
            piece_of_list = BANK // PIECE + piece
            pick(picked[1], in_half, entries(offs_sb, piece_of_list, PIECE))
            for t in range(PACK):
                product(inf[t][1][:, in_half], w1_mx[t // 2], span(t % 2, P), picked[1], in_half)
                nc.scalar.activation(log_sig[t][:, span(piece_of_list, PIECE)], inf[t][1][:, in_half], ACT.Sigmoid, scale=-1.0)

        w2_packed = [sbuf("w2_packed%d" % a, [P, 2 * P * PACK], BF16) for a in range(PAIRS)]
        for a in range(PAIRS):
            deal(w2_packed[a], w2_raw, a)
        w3_packed = sbuf("w3_packed", [P, N * PACK], BF16)
        nc.vector.tensor_copy(w3_packed[:].rearrange("p (c r) -> p c r", r=PACK), w3_raw[:].rearrange("p r c -> p c r"))
        w3_mx = quantize("w3_mx", w3_packed)
        unit_neg = sbuf("unit_neg", [P, PACK], F32)
        nc.vector.tensor_scalar(unit_neg[:], unit_sb[:], -1.0, None, ALU.mult)

        load = [sbuf("load%d" % t, [P, S], F32) for t in range(PACK)]
        for t in range(PACK):
            nc.scalar.activation(log_sig[t][:], log_sig[t][:], ACT.Ln, bias=floor_col[:])
        dose = [sbuf("dose%d" % t, [P, S], F32) for t in range(PACK)]
        log_dose = [sbuf("log_dose%d" % t, [P, S], F32) for t in range(PACK)]
        fetched = {t: sbuf("fetched%d" % t, [P, S], F32) for t in SCALAR_LANES}

        def softplus(t):
            for h in range(HALVES):
                cols = span(h, BANK)
                nc.vector.scalar_tensor_tensor(load[t][:, cols], log_sig[t][:, cols], -1.0, inf[t][h][:], ALU.mult, ALU.max)

        def fetch(t):
            for h in range(HALVES):
                cols = span(h, BANK)
                looked_up = load[t][:].indirect(entries(exp_sb, h, BANK))
                if t in SCALAR_LANES:
                    nc.scalar.activation(fetched[t][:, cols], looked_up, ACT.Copy)
                else:
                    nc.vector.tensor_tensor(dose[t][:, cols], looked_up, mask_sb[t // 2][:, t % 2, cols], ALU.mult)

        def apply_mask(t):
            nc.vector.tensor_tensor(dose[t][:], fetched[t][:], mask_sb[t // 2][:, t % 2, :], ALU.mult)

        def log_one_plus(t):
            nc.scalar.activation(log_dose[t][:], dose[t][:], ACT.Ln, bias=one_col[:])

        softplus(0)
        softplus(1)
        fetch(0)
        fetch(1)
        log_one_plus(0)
        softplus(2)
        softplus(3)
        fetch(3)
        apply_mask(1)
        fetch(2)
        apply_mask(3)
        for t in range(1, PACK):
            log_one_plus(t)

        w2_mx = [quantize("w2_mx0", w2_packed[0], tag="fetched3"), quantize("w2_mx1", w2_packed[1], tag="w2_packed0")]
        inv_dose_tags = ["dose%d" % (PACK - 1)] + ["log_dose%d" % t for t in range(PACK - 1)]
        tanh_sus = [sbuf("tanh_sus%d" % t, [P, S], F32) for t in range(PACK)]
        haz = [sbuf("haz%d" % t, [P, S], F32) for t in range(PACK)]
        for t in range(PACK):
            inv_dose = sbuf("inv_dose%d" % t, [P, S], F32, tag=inv_dose_tags[t])
            nc.scalar.activation(inv_dose[:], log_dose[t][:], ACT.Exp, scale=-1.0)
            nc.vector.tensor_scalar(
                haz[t][:].rearrange("p (d v) -> p v d", d=D),
                inv_dose[:].rearrange("p (v d) -> p v d", d=D),
                0.5,
                -0.5,
                ALU.mult,
                ALU.add,
            )
            for h in range(HALVES):
                sus = bank("sus%d%d" % (t, h), HALVES * t + h)
                product(sus[:], w2_mx[t // 2], span(t % 2, P), picked[h], whole)
                nc.scalar.activation(
                    member_major(tanh_sus[t])[:, :, span(h, P)], sus[:].rearrange("p (v d) -> p d v", d=D), ACT.Tanh, scale=0.5
                )

        def turned_lane(pair_banks, t):
            return pair_banks[t // 2][:, span(t % 2, V)]

        def turned_sum(total, values, b):
            for d in range(D):
                nc.tensor.matmul(
                    total[:, span(b, P)],
                    member_major(values)[:, d, span(b, P)],
                    ident[:],
                    start=(d == 0),
                    stop=(d == D - 1),
                    is_transpose=True,
                )

        toth = [bank("toth%d" % a, a) for a in range(PAIRS)]
        square_sum = [bank("square_sum%d" % a, PAIRS + a) for a in range(PAIRS)]
        for t in range(PACK):
            for b in range(BLOCKS):
                block = member_major(haz[t])[:, :, span(b, P)]
                nc.vector.scalar_tensor_tensor(block, member_major(tanh_sus[t])[:, :, span(b, P)], 1.0, block, ALU.add, ALU.mult)
                turned_sum(turned_lane(toth, t), haz[t], b)
        square = [sbuf("square%d" % t, [P, S], F32) for t in range(PACK)]
        for t in range(PACK):
            nc.vector.tensor_tensor(square[t][:], haz[t][:], haz[t][:], ALU.mult)
            for b in range(BLOCKS):
                turned_sum(turned_lane(square_sum, t), square[t], b)

        log_toth = sbuf("log_toth", [P, PACK * V], F32)
        conc = sbuf("conc", [P, PACK * V], F32)
        for a in range(PAIRS):
            nc.scalar.activation(log_toth[:, span(a, 2 * V)], toth[a][:], ACT.Ln, bias=one_col[:], scale=-10.0)
        nc.scalar.activation(conc[:], log_toth[:], ACT.Exp, scale=-2.0)
        escape = sbuf("escape", [P, PACK * V], F32, tag="log_toth")
        for a in range(PAIRS):
            nc.scalar.activation(escape[:, span(a, 2 * V)], toth[a][:], ACT.Exp)
        back = []
        for t in range(PACK):
            lane = span(t, V)
            nc.vector.scalar_tensor_tensor(conc[:, lane], conc[:, lane], 100.0, turned_lane(square_sum, t), ALU.mult, ALU.mult)
            back.append(bank("back%d" % t, 2 * PAIRS + t))
            for term_number, term in enumerate((conc, escape)):
                for b in range(BLOCKS):
                    nc.tensor.matmul(
                        back[t][:, span(b, P)],
                        term[:, span(BLOCKS * t + b, P)],
                        ident[:],
                        start=(term_number == 0 and b == 0),
                        stop=(term_number == 1 and b == BLOCKS - 1),
                        is_transpose=True,
                    )

        lane_values = [sbuf("lane_values%d" % h, [P, PACK, PART], BF16) for h in range(U // PART)]
        hid_packed = [sbuf("hid_packed%d" % h, [P, PART * PACK], BF16) for h in range(U // PART)]

        def look_up(t, h, on_scalar):
            looked_up = square[t][:].indirect(entries(per_sb, h, PART))
            if on_scalar:
                nc.scalar.activation(lane_values[h][:, t, :], looked_up, ACT.Copy)
            else:
                nc.vector.tensor_copy(lane_values[h][:, t, :], looked_up)

        def interleave(h):
            nc.vector.tensor_copy(
                hid_packed[h][:].rearrange("p (c i t) -> p c t i", i=LINE, t=PACK),
                lane_values[h][:].rearrange("p t (c i) -> p c t i", i=LINE),
            )

        def last_product(h):
            hid_mx = quantize("hid_mx%d" % h, hid_packed[h])
            regions = bank("regions%d" % h, h)
            product(regions[:, 0:PART], w3_mx, span(0, N), hid_mx, span(0, PART))
            result = sbuf("result%d" % h, [P, PART], F32)
            nc.scalar.copy(result[:], regions[:, 0:PART])
            nc.sync.dma_start(out[:, span(h, PART)], result[:])

        for t in range(PACK):
            factor, offset = unit_neg[:, t : t + 1], unit_sb[:, t : t + 1]
            if t % 2 == 0:
                nc.scalar.activation(square[t][:, 0:V], back[t][:, 0:V], ACT.Identity, bias=offset, scale=factor)
            else:
                nc.vector.tensor_scalar(square[t][:, 0:V], back[t][:, 0:V], factor, offset, ALU.mult, ALU.add)
            look_up(t, 0, t % 2 == 0)
        interleave(0)
        for t in (0, 2, 1):
            look_up(t, 1, True)
        look_up(PACK - 1, 1, False)
        last_product(0)
        interleave(1)
        last_product(1)
